import numpy as np
import ml_dtypes


def mxq(x, axis, fmt="e4m3"):
    dtype, down = {"e4m3": (ml_dtypes.float8_e4m3fn, 7), "e5m2": (ml_dtypes.float8_e5m2, 14)}[fmt]
    v = np.moveaxis(np.asarray(x, np.float32).astype(ml_dtypes.bfloat16).astype(np.float64), axis, -1)
    blocks = v.reshape(v.shape[:-1] + (-1, 32))
    amax = np.abs(blocks).max(-1, keepdims=True)
    byte = np.maximum(np.where(amax > 0, np.frexp(amax)[1] - 1 + 127, 0) - down, 1)
    scale = np.exp2(byte - 127.0)
    codes = (blocks / scale).astype(np.float32).astype(dtype).astype(np.float64)
    return np.moveaxis((codes * scale).reshape(v.shape), -1, axis)


WIDE = False


def mx_kscale(k):
    if not WIDE:
        return np.ones(k)
    levels = np.array([30, -30])
    if k % 512:
        return np.exp2(np.random.permutation(np.resize(levels, k // 32))).repeat(32)
    a = np.empty((k // 512, 16))
    for p in range(k // 512):
        a[p, :8] = np.random.permutation(np.resize(levels, 8))
        for g in range(8):
            far = levels[np.abs(levels - a[p, g]) >= 10]
            a[p, g + 8] = far[np.random.randint(len(far))]
    return np.exp2(a.ravel()).repeat(32)


def f64(x):
    return np.asarray(x).astype(np.float64)


def striped(idx):
    return np.tile(np.asarray(idx).reshape(-1, 16).T, (8, 1)).astype(np.uint16)


def unstriped(offs):
    return offs[:16].T.reshape(-1).astype(np.int64)


E2M1 = np.array([0.0, 0.5, 1.0, 1.5, 2.0, 3.0, 4.0, 6.0, -0.0, -0.5, -1.0, -1.5, -2.0, -3.0, -4.0, -6.0])


def pack_weight(w, fmt):
    k, n = w.shape
    w = f64(np.asarray(w, np.float32).astype(ml_dtypes.bfloat16)).reshape(k // 32, 32, n)
    amax = np.abs(w).max(1)
    if fmt in ("e4m3", "e5m2"):
        byte = np.frexp(amax)[1] - 1 + 127 - (7 if fmt == "e4m3" else 14)
    else:
        mant, ex = np.frexp(amax / 6.0)
        byte = np.where(mant > 0.5, ex, ex - 1) + 127
    byte = np.clip(np.where(amax > 0, byte, 1), 1, 254)
    scaled = (w * np.exp2(127.0 - byte)[:, None, :]).reshape(k, n).astype(np.float32)
    by_word = np.ascontiguousarray(scaled.reshape(k // 512, 128, 4, n).transpose(0, 1, 3, 2))
    if fmt in ("e4m3", "e5m2"):
        words = by_word.astype(ml_dtypes.float8_e4m3fn if fmt == "e4m3" else ml_dtypes.float8_e5m2).view(np.uint8)
    else:
        c = by_word.astype(ml_dtypes.float4_e2m1fn).view(np.uint8) & 0xF
        words = (c[..., 0::2] | (c[..., 1::2] << 4)).reshape(k // 512, 128, 2 * n)
    return np.ascontiguousarray(words), np.ascontiguousarray(byte.astype(np.uint8).reshape(k // 512, 16, n))


def unpack_weight(words, scales, fmt):
    g, _, n = scales.shape
    words = np.ascontiguousarray(words).reshape(g, 128, n, -1)
    if fmt in ("e4m3", "e5m2"):
        vals = words.view(ml_dtypes.float8_e4m3fn if fmt == "e4m3" else ml_dtypes.float8_e5m2).astype(np.float64)
    else:
        nib = np.empty((g, 128, n, 4), np.uint8)
        nib[..., 0::2] = words & 0xF
        nib[..., 1::2] = words >> 4
        vals = E2M1[nib]
    vals = vals * np.repeat(np.exp2(scales.astype(np.float64) - 127.0), 8, axis=1)[..., None]
    return vals.transpose(0, 1, 3, 2).reshape(g * 512, n)


def sgn(shape):
    return np.random.uniform(0.5, 2.0, shape) * np.where(np.random.standard_normal(shape) < 0, -1.0, 1.0)


K, T, J, F, Z, Q, R, C, O, N = 512, 1024, 256, 512, 1024, 128, 512, 512, 256, 256


def setup_inputs():
    n = np.random.standard_normal
    idx = np.random.permutation(T)[:J]
    idx2 = np.random.permutation(Z)[:J]
    idx3 = np.random.permutation(C)[:J]
    idx4 = np.random.permutation(C)[:J]
    idx5 = np.random.permutation(C)[:O]
    idx6 = np.random.permutation(C)[:O]
    fk = mx_kscale(K)
    ff = mx_kscale(F)
    fr = mx_kscale(R)
    xtp = pack_weight(n((K, T)) / fk[:, None], "e2m1")
    xop = pack_weight(n((F, Z)) / ff[:, None], "e5m2")
    wp = pack_weight(n((K, Q)) * 1 / np.sqrt(K) * fk[:, None], "e5m2")
    w2p = pack_weight(n((F, Q)) * 1 / np.sqrt(F) * ff[:, None], "e4m3")
    wbp = pack_weight(n((R, N)) * 1 / np.sqrt(R) / fr[:, None], "e4m3")
    return {
        "xt_words": xtp[0],
        "xt_scales": xtp[1],
        "xo_words": xop[0],
        "xo_scales": xop[1],
        "w_words": wp[0],
        "w_scales": wp[1],
        "w2_words": w2p[0],
        "w2_scales": w2p[1],
        "sa": (np.random.uniform(0.5, 1.6, (Q, 1)) * fr[::4, None]).astype(np.float32),
        "sb": (sgn((Q, 1)) * fr[::4, None]).astype(np.float32),
        "wb_words": wbp[0],
        "wb_scales": wbp[1],
        "offs": striped(idx),
        "offs2": striped(idx2),
        "offs3": striped(idx3),
        "offs4": striped(idx4),
        "offs5": striped(idx5),
        "offs6": striped(idx6),
    }


def reference(xt_words, xt_scales, xo_words, xo_scales, w_words, w_scales, w2_words, w2_scales, sa, sb, wb_words, wb_scales, offs, offs2, offs3, offs4, offs5, offs6):
    idx = unstriped(offs)
    idx2 = unstriped(offs2)
    idx3 = unstriped(offs3)
    idx4 = unstriped(offs4)
    idx5 = unstriped(offs5)
    idx6 = unstriped(offs6)
    xtu = unpack_weight(xt_words, xt_scales, "e2m1")
    xou = unpack_weight(xo_words, xo_scales, "e5m2")
    wu = unpack_weight(w_words, w_scales, "e5m2")
    w2u = unpack_weight(w2_words, w2_scales, "e4m3")
    wbu = unpack_weight(wb_words, wb_scales, "e4m3")
    xtidxg = xtu[:, idx]
    a = wu.T @ xtidxg
    xoidx2g = xou[:, idx2]
    b = w2u.T @ xoidx2g
    pa = np.zeros((Q, C))
    pa[:, idx3] = a * f64(sa)
    pb = np.zeros((Q, C))
    pb[:, idx4] = b * f64(sb)
    v0 = pa[:, idx5]
    v1 = pb[:, idx5]
    v2 = pa[:, idx6]
    v3 = pb[:, idx6]
    hid = np.stack([v0, v1, v2, v3], axis=1).reshape(R, O)
    hidq = mxq(hid, 0, "e5m2")
    p = wbu.T @ hidq
    return p

from contextlib import ExitStack

import concourse.mybir as mybir

F32 = mybir.dt.float32
BF16 = mybir.dt.bfloat16
I32 = mybir.dt.int32
U32 = mybir.dt.uint32
U16 = mybir.dt.uint16
U8 = mybir.dt.uint8
E4M3 = mybir.dt.float8_e4m3fn_x4
E5M2 = mybir.dt.float8_e5m2_x4
E2M1 = mybir.dt.float4_e2m1fn_x4
COPY = mybir.ActivationFunctionType.Copy

P = 128
T = 1024
J = 256
C = 512
O = 256
N = 256
HALF = 128
FLOPS = 2 * 512 * 128 * 256 * 2 + 2 * 512 * 256 * 256


def tile_list_fourreads_kernel(tc, xt_words, xt_scales, xo_words, xo_scales, w_words, w_scales, w2_words, w2_scales,
                                    sa, sb, wb_words, wb_scales, offs, offs2, offs3, offs4, offs5, offs6, out):
    nc = tc.nc
    with ExitStack() as ctx:
        lists = ctx.enter_context(tc.tile_pool(name="lists", bufs=1))
        sb_pool = ctx.enter_context(tc.tile_pool(name="work", bufs=1))
        psum = ctx.enter_context(tc.psum_pool(name="psum", bufs=1))

        def tile(name, shape, dtype):
            return sb_pool.tile(shape, dtype, name=name, align_bytes=64)

        def load_list(name, src):
            t = lists.tile([P, 16], U16, name=name)
            nc.sync.dma_start(t[:], src)
            return t

        def zero_plane(name, width):
            t = tile(name, [P, width], U8)
            nc.vector.memset(t[:].bitcast(I32), 0)
            return t

        def load_words(queue, name, src, width, dtype):
            t = tile(name, [P, width], dtype)
            queue.dma_start(t[:].bitcast(I32), src.bitcast(I32))
            return t

        def load_scale_rows(queue, name, scales, width):
            t = tile(name, [4, 4, width // 4], I32)
            queue.dma_start(t[:], scales[0].bitcast(I32).rearrange("(q r) c -> r q c", r=4))
            return t

        def place_scale_rows(plane, rows):
            for q in range(4):
                nc.vector.tensor_copy(plane[32 * q : 32 * q + 4, :].bitcast(I32), rows[:, q, :])

        def fp8_words(words):
            return words[0].rearrange("p n t -> p (n t)")

        xt_plane = zero_plane("xt_plane", T)
        w_plane = zero_plane("w_plane", P)

        l1 = load_list("l1", offs)
        w_rows = load_scale_rows(nc.sync, "w_rows", w_scales, P)
        xt_win = load_words(nc.sync, "xt_win", xt_words[0], T, U16)
        w_codes = load_words(nc.sync, "w_codes", fp8_words(w_words), P, U32)
        for q in range(4):
            nc.scalar.dma_start(xt_plane[32 * q : 32 * q + 4, :].bitcast(I32), xt_scales[0, 4 * q : 4 * q + 4, :].bitcast(I32))
        l3 = load_list("l3", offs3)
        sa_t = tile("sa_t", [P, 1], F32)
        nc.sync.dma_start(sa_t[:], sa)
        l2 = load_list("l2", offs2)
        xo_rows = load_scale_rows(nc.sync, "xo_rows", xo_scales, T)
        xo_win = load_words(nc.sync, "xo_win", fp8_words(xo_words), T, U32)
        l5 = load_list("l5", offs5)
        w2_rows = load_scale_rows(nc.sync, "w2_rows", w2_scales, P)
        w2_codes = load_words(nc.sync, "w2_codes", fp8_words(w2_words), P, U32)
        l6 = load_list("l6", offs6)
        l4 = load_list("l4", offs4)
        sb_t = tile("sb_t", [P, 1], F32)
        nc.sync.dma_start(sb_t[:], sb)
        wb_rows = load_scale_rows(nc.sync, "wb_rows", wb_scales, N)
        wb_codes = load_words(nc.sync, "wb_codes", fp8_words(wb_words), N, U32)

        pa = tile("pa", [P, C], F32)
        nc.vector.memset(pa[:], 0.0)
        pb = tile("pb", [P, C], F32)
        nc.vector.memset(pb[:], 0.0)
        xo_plane = zero_plane("xo_plane", T)
        w2_plane = zero_plane("w2_plane", P)
        wb_plane = zero_plane("wb_plane", N)

        place_scale_rows(w_plane, w_rows)
        xt_gs = tile("xt_gs", [P, J], U8)
        nc.vector.tensor_copy(xt_gs[:], xt_plane[:].indirect(l1[:]))
        xt_gw = tile("xt_gw", [P, J], U16)
        nc.vector.tensor_copy(xt_gw[:], xt_win[:].indirect(l1[:]))
        a_ps = psum.tile([P, J], F32, name="a_ps")
        nc.tensor.matmul_mx(out=a_ps[:], lhsT=w_codes[:].bitcast(E5M2), lhsT_scale=w_plane[:],
                            rhs=xt_gw[:].bitcast(E2M1), rhs_scale=xt_gs[:], start=True, stop=True)
        a_sb = tile("a_sb", [P, J], F32)
        nc.scalar.activation(a_sb[:], a_ps[:], COPY)
        nc.scalar.activation(pa[:].indirect(l3[:]), a_sb[:], COPY, scale=sa_t[:])

        place_scale_rows(xo_plane, xo_rows)
        place_scale_rows(w2_plane, w2_rows)
        xo_gs = tile("xo_gs", [P, J], U8)
        nc.vector.tensor_copy(xo_gs[:], xo_plane[:].indirect(l2[:]))
        xo_gw = tile("xo_gw", [P, J], U32)
        nc.vector.tensor_copy(xo_gw[:], xo_win[:].indirect(l2[:]))
        b_ps = psum.tile([P, J], F32, name="b_ps")
        nc.tensor.matmul_mx(out=b_ps[:], lhsT=w2_codes[:].bitcast(E4M3), lhsT_scale=w2_plane[:],
                            rhs=xo_gw[:].bitcast(E5M2), rhs_scale=xo_gs[:], start=True, stop=True)
        b_sb = tile("b_sb", [P, J], F32)
        nc.vector.tensor_copy(b_sb[:], b_ps[:])
        place_scale_rows(wb_plane, wb_rows)

        hid = [tile("hid%d" % h, [P, 4 * HALF], BF16) for h in range(2)]

        def read(board, lst, slot):
            for h in range(2):
                nc.scalar.activation(hid[h][:, slot : 4 * HALF : 4], board[:].indirect(lst[:, 8 * h : 8 * h + 8]), COPY)

        read(pa, l5, 0)
        nc.scalar.activation(pb[:].indirect(l4[:]), b_sb[:], COPY, scale=sb_t[:])
        read(pa, l6, 2)
        read(pb, l5, 1)
        read(pb, l6, 3)

        hq = [tile("hq%d" % h, [P, HALF], U32) for h in range(2)]
        hs = [tile("hs%d" % h, [P, HALF], U8) for h in range(2)]
        for h in range(2):
            nc.vector.quantize_mx(out=hq[h][:].bitcast(E5M2), scales=hs[h][:], in_=hid[h][:])

        def product(dst, m, h):
            nc.tensor.matmul_mx(out=dst, lhsT=wb_codes[:, m * P : (m + 1) * P].bitcast(E4M3),
                                lhsT_scale=wb_plane[:, m * P : (m + 1) * P],
                                rhs=hq[h][:].bitcast(E5M2), rhs_scale=hs[h][:], start=True, stop=True)

        o0_ps = psum.tile([P, 2, HALF], F32, name="o0_ps")
        for m in range(2):
            product(o0_ps[:, m, :], m, 0)
        o0 = tile("o0", [P, 2, HALF], F32)
        nc.scalar.copy(o0[:], o0_ps[:])
        nc.sync.dma_start(out.rearrange("(m p) o -> p m o", p=P)[:, :, 0:HALF], o0[:])
        for m in range(2):
            o1_ps = psum.tile([P, HALF], F32, name="o1_ps%d" % m)
            product(o1_ps[:], m, 1)
            o1 = tile("o1_%d" % m, [P, HALF], F32)
            if m == 0:
                nc.vector.tensor_copy(o1[:], o1_ps[:])
                nc.sync.dma_start(out[0:P, HALF:O], o1[:])
            else:
                nc.scalar.copy(o1[:], o1_ps[:])
                nc.scalar.dma_start(out[P:N, HALF:O], o1[:])
